import numpy as np
import ml_dtypes


def mxq(x, axis, fmt="e4m3"):
    dtype, down = {"e4m3": (ml_dtypes.float8_e4m3fn, 7), "e5m2": (ml_dtypes.float8_e5m2, 14)}[fmt]
    v = np.moveaxis(np.asarray(x, np.float32).astype(ml_dtypes.bfloat16).astype(np.float64), axis, -1)
    blocks = v.reshape(v.shape[:-1] + (-1, 32))
    amax = np.abs(blocks).max(-1, keepdims=True)
    byte = np.maximum(np.where(amax > 0, np.frexp(amax)[1] - 1 + 127, 0) - down, 1)
    scale = np.exp2(byte - 127.0)
    codes = (blocks / scale).astype(np.float32).astype(dtype).astype(np.float64)
    return np.moveaxis((codes * scale).reshape(v.shape), -1, axis)


WIDE = False


def mx_kscale(k):
    if not WIDE:
        return np.ones(k)
    levels = np.array([10, -10, 5, -5, 0])
    if k % 512:
        return np.exp2(np.random.permutation(np.resize(levels, k // 32))).repeat(32)
    a = np.empty((k // 512, 16))
    for p in range(k // 512):
        a[p, :8] = np.random.permutation(np.resize(levels, 8))
        for g in range(8):
            far = levels[np.abs(levels - a[p, g]) >= 10]
            a[p, g + 8] = far[np.random.randint(len(far))]
    return np.exp2(a.ravel()).repeat(32)


def f64(x):
    return np.asarray(x).astype(np.float64)


def striped(idx):
    return np.tile(idx.reshape(-1, 16).T, (8, 1)).astype(np.uint16)


def unstriped(offs):
    return offs[:16].T.reshape(-1).astype(np.int64)


E2M1 = np.array([0.0, 0.5, 1.0, 1.5, 2.0, 3.0, 4.0, 6.0, -0.0, -0.5, -1.0, -1.5, -2.0, -3.0, -4.0, -6.0])


def pack_weight(w, fmt):
    k, n = w.shape
    w = f64(np.asarray(w, np.float32).astype(ml_dtypes.bfloat16)).reshape(k // 32, 32, n)
    amax = np.abs(w).max(1)
    if fmt == "e4m3":
        byte = np.frexp(amax)[1] - 1 + 127 - 7
    else:
        mant, ex = np.frexp(amax / 6.0)
        byte = np.where(mant > 0.5, ex, ex - 1) + 127
    byte = np.clip(np.where(amax > 0, byte, 1), 1, 254)
    scaled = (w * np.exp2(127.0 - byte)[:, None, :]).reshape(k, n).astype(np.float32)
    by_word = np.ascontiguousarray(scaled.reshape(k // 512, 128, 4, n).transpose(0, 1, 3, 2))
    if fmt == "e4m3":
        words = by_word.astype(ml_dtypes.float8_e4m3fn).view(np.uint8)
    else:
        c = by_word.astype(ml_dtypes.float4_e2m1fn).view(np.uint8) & 0xF
        words = (c[..., 0::2] | (c[..., 1::2] << 4)).reshape(k // 512, 128, 2 * n)
    return np.ascontiguousarray(words), np.ascontiguousarray(byte.astype(np.uint8).reshape(k // 512, 16, n))


def unpack_weight(words, scales, fmt):
    g, _, n = scales.shape
    words = np.ascontiguousarray(words).reshape(g, 128, n, -1)
    if fmt == "e4m3":
        vals = words.view(ml_dtypes.float8_e4m3fn).astype(np.float64)
    else:
        nib = np.empty((g, 128, n, 4), np.uint8)
        nib[..., 0::2] = words & 0xF
        nib[..., 1::2] = words >> 4
        vals = E2M1[nib]
    vals = vals * np.repeat(np.exp2(scales.astype(np.float64) - 127.0), 8, axis=1)[..., None]
    return vals.transpose(0, 1, 3, 2).reshape(g * 512, n)


def gelu(v):
    return 0.5 * v * (1.0 + np.tanh(np.sqrt(2.0 / np.pi) * (v + 0.044715 * v**3)))


def striped8(idx):
    return np.concatenate([v.reshape(-1, 16).T for v in idx]).astype(np.uint16)


def unstriped8(offs):
    return np.stack([offs[16 * g:16 * g + 16].T.reshape(-1) for g in range(8)]).astype(np.int64)


def heads(h, wgt, idx8):
    r = np.arange(h.shape[0])
    return wgt[r // 4 % 128] * h[r[:, None], idx8[r % 512 // 64]]


def put_heads(h, wgs, idx8, t2):
    r = np.arange(h.shape[0])
    page = np.zeros((h.shape[0], t2))
    page[r[:, None], idx8[r % 512 // 64]] = wgs[r // 4 % 128] * h
    return page


K, H, N, T, S, P, T2 = 1024, 1024, 512, 4096, 1024, 512, 1024


def setup_inputs():
    n = np.random.standard_normal
    s = mx_kscale(K)[:, None]
    u = mx_kscale(H)[:, None]
    d = {}
    d["tab_words"], d["tab_scales"] = pack_weight(n((K, T)) * s, "e4m3")
    d["offs"] = striped(np.random.permutation(T)[:S])
    d["w1"] = (n((K, H)) / K**0.5 / s).astype(np.float32)
    d["w2_words"], d["w2_scales"] = pack_weight(n((K, H)) / K**0.5 / s, "e2m1")
    d["gain"] = (np.exp(0.3 * n(H)) * u[:, 0]**2).astype(np.float32)
    d["offs2"] = striped8(np.stack([np.random.permutation(S)[:P] for _ in range(8)]))
    d["wgt"] = np.repeat(np.random.uniform(0.5, 2.0, (8, P)), 16, axis=0).astype(np.float32)
    d["lift"] = (np.random.uniform(0.2, 0.6, H) * u[:, 0]**2).astype(np.float32)
    d["w3_words"], d["w3_scales"] = pack_weight(n((H, N)) / H**0.5 / u, "e4m3")
    d["base"] = n((N, P)).astype(np.float32)
    d["offs3"] = striped8(np.stack([np.random.permutation(T2)[:P] for _ in range(8)]))
    d["wgo"] = np.repeat(np.random.uniform(0.5, 2.0, (8, P)), 16, axis=0).astype(np.float32)
    return d


def reference(tab_words, tab_scales, offs, w1, w2_words, w2_scales, gain, offs2, wgt,
              lift, w3_words, w3_scales, base, offs3, wgo):
    v = unpack_weight(tab_words, tab_scales, "e4m3")[:, unstriped(offs)]
    w2 = unpack_weight(w2_words, w2_scales, "e2m1")
    w3 = unpack_weight(w3_words, w3_scales, "e4m3")
    a = mxq(f64(w1), 0, "e4m3").T @ v
    b = w2.T @ v
    h = f64(gain)[:, None] * np.square(a - b)
    x = heads(h, f64(wgt), unstriped8(offs2))
    z = mxq(np.sqrt(x + f64(lift)[:, None]), 0, "e4m3")
    y = (w3.T @ z) - f64(base)
    return put_heads(y, f64(wgo), unstriped8(offs3), T2)

@@ -1,0 +1,287 @@
+from contextlib import ExitStack
+
+import concourse.mybir as mybir
+
+K, H, N, T, S, P, T2 = 1024, 1024, 512, 4096, 1024, 512, 1024
+FLOPS = 2 * 2 * K * H * S + 2 * H * N * P
+
+F32 = mybir.dt.float32
+BF16 = mybir.dt.bfloat16
+I32 = mybir.dt.int32
+U32 = mybir.dt.uint32
+U16 = mybir.dt.uint16
+U8 = mybir.dt.uint8
+E4M3 = mybir.dt.float8_e4m3fn_x4
+E2M1 = mybir.dt.float4_e2m1fn_x4
+ACT = mybir.ActivationFunctionType
+ALU = mybir.AluOpType
+
+PARTS = 128
+BANK = 512
+HALF = P // 2
+
+
+def tile_list_lens_fit_register_kernel(tc, tab_words, tab_scales, offs, w1, w2_words, w2_scales, gain,
+                                                 offs2, wgt, lift, w3_words, w3_scales, base, offs3, wgo, out):
+    nc = tc.nc
+    with ExitStack() as ctx:
+        keep = ctx.enter_context(tc.tile_pool(name="keep", bufs=1))
+        ring = ctx.enter_context(tc.tile_pool(name="ring", bufs=4))
+        early = ctx.enter_context(tc.tile_pool(name="early", bufs=1))
+        psum = ctx.enter_context(tc.psum_pool(name="psum", bufs=1))
+
+        def held(shape, dtype, name, tag=None):
+            return keep.tile(shape, dtype, name=name, tag=tag or name, align_bytes=64)
+
+        def staged(shape, dtype, name, a):
+            return early.tile(shape, dtype, name=name, tag="stage%d" % a, offset=40960 * a, align_bytes=64)
+
+        scan_list = held([PARTS, S // 16], U16, "scan_list")
+        pick_lists = held([PARTS, P // 16], U16, "pick_lists")
+        file_lists = held([PARTS, P // 16], U16, "file_lists")
+
+        tab_sc = staged([PARTS, T], U8, "tab_sc", 1)
+        w_sc = held([PARTS, H], U8, "w_sc")
+        v_sc1 = held([PARTS, S], U8, "v_sc1")
+        w2_sc1 = held([PARTS, H], U8, "w2_sc1")
+        pages = [held([PARTS, T2], F32, "page%d" % i) for i in range(4)]
+        nc.vector.memset(tab_sc[:].bitcast(I32), 0)
+        nc.vector.memset(w_sc[:].bitcast(I32), 0)
+        nc.vector.memset(v_sc1[:].bitcast(I32), 0)
+        nc.vector.memset(w2_sc1[:].bitcast(I32), 0)
+
+        nc.sync.dma_start(scan_list[:], offs)
+        nc.sync.dma_start(pick_lists[:], offs2)
+        nc.sync.dma_start(file_lists[:], offs3)
+        w2_raw = early.tile([PARTS, 2, 2 * H], U8, name="w2_raw", offset=6144, align_bytes=64)
+        nc.sync.dma_start(w2_raw[:].bitcast(I32), w2_words.rearrange("a p c -> p a c").bitcast(I32))
+        tab = {}
+        w1_raw = {}
+
+        def load_tab(a):
+            tab[a] = early.tile([PARTS, T], U32, name="tab%d" % a, offset=24576 - 16384 * a, align_bytes=64)
+            nc.sync.dma_start(tab[a][:].bitcast(I32), tab_words[a].rearrange("p t i -> p (t i)").bitcast(I32))
+
+        def load_w1(a, b):
+            w1_raw[a, b] = staged([PARTS, 4, BANK], F32, "w1_raw%d%d" % (a, b), a)
+            rows = w1[512 * a:512 * a + 512, 512 * b:512 * b + 512]
+            nc.sync.dma_start(w1_raw[a, b][:], rows.rearrange("(p j) c -> p j c", j=4))
+
+        tab_rows = tab_scales.rearrange("a (q r) t -> r q a t", r=4)
+        w2_rows = w2_scales.rearrange("a (q r) c -> r q a c", r=4)
+        for r in range(4):
+            nc.scalar.dma_start(tab_sc[r:PARTS:16, :].bitcast(I32), tab_rows[r].bitcast(I32))
+        load_tab(0)
+        gain_t = held([PARTS, 2, 4], F32, "gain_t")
+        lift_t = held([PARTS, 2, 4], F32, "lift_t")
+        nc.gpsimd.dma_start(gain_t[:], gain.rearrange("(b p i) -> p b i", b=2, i=4))
+        for r in range(4):
+            nc.scalar.dma_start(w_sc[r:PARTS:16, :].bitcast(I32), w2_rows[r].bitcast(I32))
+        nc.gpsimd.dma_start(lift_t[:], lift.rearrange("(b p i) -> p b i", b=2, i=4))
+
+        for i in range(4):
+            nc.vector.memset(pages[i][:], 0.0)
+
+        root_gain = held([PARTS, 8], F32, "root_gain")
+        nc.scalar.activation(root_gain[:], gain_t[:].rearrange("p b i -> p (b i)"), ACT.Sqrt)
+
+        v_sc0 = held([PARTS, S], U8, "v_sc0")
+        nc.vector.tensor_copy(v_sc0[:], tab_sc[:].indirect(scan_list[:]))
+        nc.scalar.dma_start(v_sc1[0:112, :].bitcast(I32), v_sc0[16:PARTS, :].bitcast(I32))
+        v_sc = [v_sc0, v_sc1]
+
+        w2_dealt = held([PARTS, 4 * 4 * PARTS * 2], U8, "w2_dealt")
+        nc.vector.tensor_copy(
+            w2_dealt[:].bitcast(U16).rearrange("p (i g m) -> p g i m", i=4, m=8),
+            w2_raw[:].rearrange("p a c -> p (a c)").bitcast(U16).rearrange("p (g m i) -> p g i m", i=4, m=8))
+        load_w1(0, 0)
+        load_tab(1)
+        load_w1(1, 0)
+        sc_dealt = held([PARTS, H], U8, "sc_dealt")
+        nc.vector.tensor_copy(
+            sc_dealt[:].rearrange("p (i g m) -> p g i m", i=4, m=16),
+            w_sc[:].rearrange("p (g m i) -> p g i m", i=4, m=16))
+        nc.scalar.dma_start(w2_sc1[0:112, :].bitcast(I32), sc_dealt[16:PARTS, :].bitcast(I32))
+        w2_sc = [sc_dealt, w2_sc1]
+        w3_sc_raw = held([PARTS, N], U8, "w3_sc_raw", "w_sc")
+        nc.vector.memset(w3_sc_raw[:].bitcast(I32), 0)
+        for q in range(4):
+            nc.sync.dma_start(w3_sc_raw[32 * q:32 * q + 8, :].bitcast(I32),
+                              w3_scales[:, 4 * q:4 * q + 4, :].bitcast(I32))
+
+        v = {}
+
+        def gather_tab(a):
+            for s in range(2):
+                v[a, s] = held([PARTS, BANK], U32, "v%d%d" % (a, s))
+                nc.vector.tensor_copy(v[a, s][:], tab[a][:].indirect(scan_list[:, 32 * s:32 * s + 32]))
+
+        w1_codes = {}
+        w1_sc = {}
+        w1_bf = {}
+
+        def cast_w1(a, b, u, on_vector):
+            w1_bf[a, b, u] = ring.tile([PARTS, 2 * PARTS * 4], BF16, name="w1_bf", align_bytes=64)
+            dst = w1_bf[a, b, u][:].rearrange("p (i m j) -> p m i j", i=2, j=4)
+            src = w1_raw[a, b][:].rearrange("p j (m i) -> p m i j", i=4)[:, :, 2 * u:2 * u + 2, :]
+            if on_vector:
+                nc.vector.tensor_scalar(dst, src, -1.0, None, ALU.mult)
+            else:
+                nc.scalar.activation(dst, src, ACT.Copy, scale=-1.0)
+
+        def quant_w1(a, b, u):
+            w1_codes[a, b, u] = held([PARTS, 2 * PARTS], U32, "w1_codes%d%d%d" % (a, b, u))
+            w1_sc[a, b, u] = held([PARTS, 2 * PARTS], U8, "w1_sc%d%d%d" % (a, b, u))
+            nc.vector.quantize_mx(w1_codes[a, b, u][:].bitcast(E4M3), w1_sc[a, b, u][:], w1_bf[a, b, u][:])
+
+        banks = {}
+
+        def pass_w2(a, b, i):
+            c = PARTS * (4 * i + 2 * a + b)
+            cs = PARTS * (2 * i + b)
+            for s in range(2):
+                if a == 0:
+                    banks[b, i, s] = psum.tile([PARTS, BANK], F32, name="bank%d" % (2 * i + s))
+                cols = slice(BANK * s, BANK * s + BANK)
+                nc.tensor.matmul_mx(banks[b, i, s][:], lhsT=w2_dealt[:, 2 * c:2 * c + 2 * PARTS].bitcast(E2M1),
+                                    lhsT_scale=w2_sc[a][:, cs:cs + PARTS], rhs=v[a, s][:].bitcast(E4M3),
+                                    rhs_scale=v_sc[a][:, cols], start=(a == 0), stop=False)
+
+        def pass_w1(a, b, i):
+            u, c = i // 2, PARTS * (i % 2)
+            for s in range(2):
+                cols = slice(BANK * s, BANK * s + BANK)
+                nc.tensor.matmul_mx(banks[b, i, s][:], lhsT=w1_codes[a, b, u][:, c:c + PARTS].bitcast(E4M3),
+                                    lhsT_scale=w1_sc[a, b, u][:, c:c + PARTS], rhs=v[a, s][:].bitcast(E4M3),
+                                    rhs_scale=v_sc[a][:, cols], start=False, stop=(a == 1))
+
+        h = {}
+        x = {}
+        z_planes = {}
+        z_codes = {}
+        z_sc = {}
+
+        def square(b, i):
+            h[b, i] = ring.tile([PARTS, S], F32, name="h", align_bytes=64)
+            for s in range(2):
+                nc.scalar.activation(h[b, i][:, BANK * s:BANK * s + BANK], banks[b, i, s][:], ACT.Square,
+                                     scale=root_gain[:, 4 * b + i:4 * b + i + 1])
+
+        def pick(b, i, halves):
+            width = HALF * len(halves)
+            picked = held([PARTS, width], F32, "x%d%d%d" % (b, i, halves[0]))
+            m0 = HALF * halves[0]
+            nc.vector.tensor_tensor(picked[:], h[b, i][:].indirect(pick_lists[:, m0 // 16:(m0 + width) // 16]),
+                                    wgt_t[:, m0:m0 + width], ALU.mult)
+            for n, c in enumerate(halves):
+                x[b, i, c] = picked[:, HALF * n:HALF * n + HALF]
+
+        def root(b, i, c):
+            if i == 0:
+                z_planes[b, c] = held([PARTS, 4, HALF], BF16, "z_planes%d%d" % (b, c))
+            nc.scalar.activation(z_planes[b, c][:, i, :], x[b, i, c], ACT.Sqrt, bias=lift_t[:, b, i:i + 1])
+
+        def quant_z(b, c):
+            z_bf = held([PARTS, HALF, 4], BF16, "z_bf%d%d" % (b, c))
+            if c == 0:
+                nc.vector.tensor_copy(z_bf[:], z_planes[b, c][:].rearrange("p i m -> p m i"))
+            else:
+                nc.scalar.copy(z_bf[:], z_planes[b, c][:].rearrange("p i m -> p m i"))
+            z_codes[b, c] = held([PARTS, HALF], U32, "z_codes%d%d" % (b, c))
+            z_sc[b, c] = held([PARTS, HALF], U8, "z_sc%d%d" % (b, c))
+            nc.vector.quantize_mx(z_codes[b, c][:].bitcast(E4M3), z_sc[b, c][:],
+                                  z_bf[:].rearrange("p m i -> p (m i)"))
+
+        def stage_one(b, i):
+            pass_w2(0, b, i)
+            pass_w1(0, b, i)
+            pass_w2(1, b, i)
+            pass_w1(1, b, i)
+            square(b, i)
+
+        gather_tab(0)
+        wgt_t = early.tile([PARTS, P], F32, name="wgt_t", offset=24576, align_bytes=64)
+        nc.sync.dma_start(wgt_t[:], wgt)
+        for u in range(2):
+            cast_w1(0, 0, u, False)
+            quant_w1(0, 0, u)
+        load_w1(0, 1)
+        gather_tab(1)
+        cast_w1(1, 0, 0, True)
+        cast_w1(1, 0, 1, False)
+        load_w1(1, 1)
+        for u in range(2):
+            quant_w1(1, 0, u)
+        for i in range(4):
+            stage_one(0, i)
+        for a in range(2):
+            for u in range(2):
+                cast_w1(a, 1, u, u == 0)
+                quant_w1(a, 1, u)
+        w3_raw = staged([PARTS, 2, N], U32, "w3_raw", 0)
+        nc.sync.dma_start(w3_raw[:].bitcast(I32), w3_words.rearrange("a p c i -> p a (c i)").bitcast(I32))
+        base_t = staged([PARTS, 4, P], F32, "base_t", 1)
+        nc.sync.dma_start(base_t[:], base.rearrange("(p i) m -> p i m", i=4))
+        for i in range(4):
+            pick(0, i, (0, 1))
+            root(0, i, 0)
+        for i in range(4):
+            stage_one(1, i)
+
+        wgo_t = held([PARTS, P], F32, "wgo_t", "w2_dealt")
+        nc.sync.dma_start(wgo_t[:], wgo)
+        w3_sc = held([PARTS, N], U8, "w3_sc")
+        nc.vector.tensor_copy(
+            w3_sc[:].rearrange("p (i g m) -> p g i m", i=4, m=16),
+            w3_sc_raw[:].rearrange("p (g m i) -> p g i m", i=4, m=16))
+        w3_dealt = held([PARTS, 2 * N], U32, "w3_dealt")
+        nc.vector.tensor_copy(
+            w3_dealt[:].bitcast(I32).rearrange("p (i g m) -> p g i m", i=4, m=4),
+            w3_raw[:].rearrange("p a c -> p (a c)").bitcast(I32).rearrange("p (g m i) -> p g i m", i=4, m=4))
+        quant_z(0, 0)
+        for i in range(4):
+            pick(1, i, (0,))
+            root(1, i, 0)
+        quant_z(1, 0)
+
+        out_rows = out.rearrange("(p i) c -> p i c", i=4)
+        y = {}
+
+        def fit(c):
+            acc = [psum.tile([PARTS, HALF], F32, name="bank%d" % (4 * c + i)) for i in range(4)]
+            for b in range(2):
+                for i in range(4):
+                    w = PARTS * (2 * i + b)
+                    nc.tensor.matmul_mx(acc[i][:], lhsT=w3_dealt[:, w:w + PARTS].bitcast(E4M3),
+                                        lhsT_scale=w3_sc[4 * b:PARTS, PARTS * i:PARTS * i + PARTS],
+                                        rhs=z_codes[b, c][:].bitcast(E4M3), rhs_scale=z_sc[b, c][:],
+                                        start=(b == 0), stop=(b == 1))
+            return acc
+
+        def depart(acc, i, c):
+            y[i, c] = held([PARTS, HALF], F32, "y%d%d" % (i, c), "z_bf11" if (i, c) == (3, 0) else None)
+            nc.vector.tensor_tensor(y[i, c][:], acc[i][:], base_t[:, i, HALF * c:HALF * c + HALF], ALU.subtract)
+
+        def file_away(i, c):
+            m0 = HALF * c
+            nc.vector.tensor_tensor(pages[i][:].indirect(file_lists[:, m0 // 16:(m0 + HALF) // 16]), y[i, c][:],
+                                    wgo_t[:, m0:m0 + HALF], ALU.mult)
+
+        acc0 = fit(0)
+        for i in range(3):
+            depart(acc0, i, 0)
+        for i in range(4):
+            pick(1, i, (1,))
+        for b in range(2):
+            for i in range(4):
+                root(b, i, 1)
+            quant_z(b, 1)
+        acc1 = fit(1)
+        depart(acc0, 3, 0)
+        for i in range(4):
+            file_away(i, 0)
+        for i in range(4):
+            depart(acc1, i, 1)
+        for i in range(4):
+            file_away(i, 1)
+            nc.sync.dma_start(out_rows[:, i, :], pages[i][:])

@@ -34,7 +34,7 @@ def tile_list_lens_fit_register_kernel(tc, tab_words, tab_scales, offs, w1, w2_w
             return keep.tile(shape, dtype, name=name, tag=tag or name, align_bytes=64)
 
         def staged(shape, dtype, name, a):
-            return early.tile(shape, dtype, name=name, tag="stage%d" % a, offset=40960 * a, align_bytes=64)
+            return early.tile(shape, dtype, name=name, tag="stage%d" % a, offset=41024 * a, align_bytes=64)
 
         scan_list = held([PARTS, S // 16], U16, "scan_list")
         pick_lists = held([PARTS, P // 16], U16, "pick_lists")
@@ -51,15 +51,15 @@ def tile_list_lens_fit_register_kernel(tc, tab_words, tab_scales, offs, w1, w2_w
         nc.vector.memset(w2_sc1[:].bitcast(I32), 0)
 
         nc.sync.dma_start(scan_list[:], offs)
-        nc.sync.dma_start(pick_lists[:], offs2)
-        nc.sync.dma_start(file_lists[:], offs3)
         w2_raw = early.tile([PARTS, 2, 2 * H], U8, name="w2_raw", offset=6144, align_bytes=64)
         nc.sync.dma_start(w2_raw[:].bitcast(I32), w2_words.rearrange("a p c -> p a c").bitcast(I32))
+        nc.sync.dma_start(pick_lists[:], offs2)
+        nc.sync.dma_start(file_lists[:], offs3)
         tab = {}
         w1_raw = {}
 
         def load_tab(a):
-            tab[a] = early.tile([PARTS, T], U32, name="tab%d" % a, offset=24576 - 16384 * a, align_bytes=64)
+            tab[a] = early.tile([PARTS, T], U32, name="tab%d" % a, offset=24640 - 16384 * a, align_bytes=64)
             nc.sync.dma_start(tab[a][:].bitcast(I32), tab_words[a].rearrange("p t i -> p (t i)").bitcast(I32))
 
         def load_w1(a, b):
@@ -72,18 +72,12 @@ def tile_list_lens_fit_register_kernel(tc, tab_words, tab_scales, offs, w1, w2_w
         for r in range(4):
             nc.scalar.dma_start(tab_sc[r:PARTS:16, :].bitcast(I32), tab_rows[r].bitcast(I32))
         load_tab(0)
-        gain_t = held([PARTS, 2, 4], F32, "gain_t")
-        lift_t = held([PARTS, 2, 4], F32, "lift_t")
-        nc.gpsimd.dma_start(gain_t[:], gain.rearrange("(b p i) -> p b i", b=2, i=4))
         for r in range(4):
             nc.scalar.dma_start(w_sc[r:PARTS:16, :].bitcast(I32), w2_rows[r].bitcast(I32))
-        nc.gpsimd.dma_start(lift_t[:], lift.rearrange("(b p i) -> p b i", b=2, i=4))
 
         for i in range(4):
             nc.vector.memset(pages[i][:], 0.0)
 
-        root_gain = held([PARTS, 8], F32, "root_gain")
-        nc.scalar.activation(root_gain[:], gain_t[:].rearrange("p b i -> p (b i)"), ACT.Sqrt)
 
         v_sc0 = held([PARTS, S], U8, "v_sc0")
         nc.vector.tensor_copy(v_sc0[:], tab_sc[:].indirect(scan_list[:]))
@@ -94,6 +88,12 @@ def tile_list_lens_fit_register_kernel(tc, tab_words, tab_scales, offs, w1, w2_w
         nc.vector.tensor_copy(
             w2_dealt[:].bitcast(U16).rearrange("p (i g m) -> p g i m", i=4, m=8),
             w2_raw[:].rearrange("p a c -> p (a c)").bitcast(U16).rearrange("p (g m i) -> p g i m", i=4, m=8))
+        gain_t = early.tile([PARTS, 2, 4], F32, name="gain_t", offset=8192)
+        lift_t = early.tile([PARTS, 2, 4], F32, name="lift_t", offset=8224)
+        nc.sync.dma_start(gain_t[:], gain.rearrange("(b p i) -> p b i", b=2, i=4))
+        nc.sync.dma_start(lift_t[:], lift.rearrange("(b p i) -> p b i", b=2, i=4))
+        root_gain = held([PARTS, 8], F32, "root_gain")
+        nc.scalar.activation(root_gain[:], gain_t[:].rearrange("p b i -> p (b i)"), ACT.Sqrt)
         load_w1(0, 0)
         load_tab(1)
         load_w1(1, 0)
@@ -136,7 +136,7 @@ def tile_list_lens_fit_register_kernel(tc, tab_words, tab_scales, offs, w1, w2_w
 
         banks = {}
 
-        def pass_w2(a, b, i):
+        def pass_w2(a, b, i, stop=False):
             c = PARTS * (4 * i + 2 * a + b)
             cs = PARTS * (2 * i + b)
             for s in range(2):
@@ -145,15 +145,15 @@ def tile_list_lens_fit_register_kernel(tc, tab_words, tab_scales, offs, w1, w2_w
                 cols = slice(BANK * s, BANK * s + BANK)
                 nc.tensor.matmul_mx(banks[b, i, s][:], lhsT=w2_dealt[:, 2 * c:2 * c + 2 * PARTS].bitcast(E2M1),
                                     lhsT_scale=w2_sc[a][:, cs:cs + PARTS], rhs=v[a, s][:].bitcast(E4M3),
-                                    rhs_scale=v_sc[a][:, cols], start=(a == 0), stop=False)
+                                    rhs_scale=v_sc[a][:, cols], start=(a == 0), stop=stop)
 
-        def pass_w1(a, b, i):
+        def pass_w1(a, b, i, stop=False):
             u, c = i // 2, PARTS * (i % 2)
             for s in range(2):
                 cols = slice(BANK * s, BANK * s + BANK)
                 nc.tensor.matmul_mx(banks[b, i, s][:], lhsT=w1_codes[a, b, u][:, c:c + PARTS].bitcast(E4M3),
                                     lhsT_scale=w1_sc[a, b, u][:, c:c + PARTS], rhs=v[a, s][:].bitcast(E4M3),
-                                    rhs_scale=v_sc[a][:, cols], start=False, stop=(a == 1))
+                                    rhs_scale=v_sc[a][:, cols], start=False, stop=stop)
 
         h = {}
         x = {}
@@ -195,12 +195,16 @@ def tile_list_lens_fit_register_kernel(tc, tab_words, tab_scales, offs, w1, w2_w
         def stage_one(b, i):
             pass_w2(0, b, i)
             pass_w1(0, b, i)
-            pass_w2(1, b, i)
-            pass_w1(1, b, i)
+            if b == 0 and i >= 2:
+                pass_w1(1, b, i)
+                pass_w2(1, b, i, stop=True)
+            else:
+                pass_w2(1, b, i)
+                pass_w1(1, b, i, stop=True)
             square(b, i)
 
         gather_tab(0)
-        wgt_t = early.tile([PARTS, P], F32, name="wgt_t", offset=24576, align_bytes=64)
+        wgt_t = early.tile([PARTS, P], F32, name="wgt_t", offset=24640, align_bytes=64)
         nc.sync.dma_start(wgt_t[:], wgt)
         for u in range(2):
             cast_w1(0, 0, u, False)

@@ -18,6 +18,7 @@ ALU = mybir.AluOpType
 
 PARTS = 128
 BANK = 512
+AT_W1, AT_TAB1, AT_W_SC, AT_TAB0, AT_SC, AT_H = 0, 8192, 24576, 25600, 41984, 54272
 HALF = P // 2
 
 
@@ -26,54 +27,58 @@ def tile_list_lens_fit_register_kernel(tc, tab_words, tab_scales, offs, w1, w2_w
     nc = tc.nc
     with ExitStack() as ctx:
         keep = ctx.enter_context(tc.tile_pool(name="keep", bufs=1))
-        ring = ctx.enter_context(tc.tile_pool(name="ring", bufs=4))
         early = ctx.enter_context(tc.tile_pool(name="early", bufs=1))
         psum = ctx.enter_context(tc.psum_pool(name="psum", bufs=1))
 
         def held(shape, dtype, name, tag=None):
             return keep.tile(shape, dtype, name=name, tag=tag or name, align_bytes=64)
 
-        def staged(shape, dtype, name, a):
-            return early.tile(shape, dtype, name=name, tag="stage%d" % a, offset=41024 * a, align_bytes=64)
+        def placed(shape, dtype, name, offset):
+            return early.tile(shape, dtype, name=name, offset=offset, align_bytes=64)
 
         scan_list = held([PARTS, S // 16], U16, "scan_list")
         pick_lists = held([PARTS, P // 16], U16, "pick_lists")
         file_lists = held([PARTS, P // 16], U16, "file_lists")
 
-        tab_sc = staged([PARTS, T], U8, "tab_sc", 1)
-        w_sc = held([PARTS, H], U8, "w_sc")
+        tab_sc = placed([PARTS, T], U8, "tab_sc", AT_SC + 4096)
         v_sc1 = held([PARTS, S], U8, "v_sc1")
         w2_sc1 = held([PARTS, H], U8, "w2_sc1")
         pages = [held([PARTS, T2], F32, "page%d" % i) for i in range(4)]
         nc.vector.memset(tab_sc[:].bitcast(I32), 0)
-        nc.vector.memset(w_sc[:].bitcast(I32), 0)
         nc.vector.memset(v_sc1[:].bitcast(I32), 0)
         nc.vector.memset(w2_sc1[:].bitcast(I32), 0)
 
         nc.sync.dma_start(scan_list[:], offs)
-        w2_raw = early.tile([PARTS, 2, 2 * H], U8, name="w2_raw", offset=6144, align_bytes=64)
-        nc.sync.dma_start(w2_raw[:].bitcast(I32), w2_words.rearrange("a p c -> p a c").bitcast(I32))
+        gain_t = placed([PARTS, 2, 16], F32, "gain_t", AT_TAB0 - 64)
+        nc.sync.dma_start(gain_t[:, :, 0:4], gain.rearrange("(b p i) -> p b i", b=2, i=4))
         nc.sync.dma_start(pick_lists[:], offs2)
         nc.sync.dma_start(file_lists[:], offs3)
+        w2_raw = placed([PARTS, 2, 2 * H], U8, "w2_raw", AT_TAB1)
+        nc.sync.dma_start(w2_raw[:].bitcast(I32), w2_words.rearrange("a p c -> p a c").bitcast(I32))
         tab = {}
         w1_raw = {}
 
         def load_tab(a):
-            tab[a] = early.tile([PARTS, T], U32, name="tab%d" % a, offset=24640 - 16384 * a, align_bytes=64)
+            tab[a] = placed([PARTS, T], U32, "tab%d" % a, (AT_TAB0, AT_TAB1)[a])
             nc.sync.dma_start(tab[a][:].bitcast(I32), tab_words[a].rearrange("p t i -> p (t i)").bitcast(I32))
 
-        def load_w1(a, b):
-            w1_raw[a, b] = staged([PARTS, 4, BANK], F32, "w1_raw%d%d" % (a, b), a)
+        def load_w1(a, b, offset):
+            w1_raw[a, b] = placed([PARTS, 4, BANK], F32, "w1_raw%d%d" % (a, b), offset)
             rows = w1[512 * a:512 * a + 512, 512 * b:512 * b + 512]
             nc.sync.dma_start(w1_raw[a, b][:], rows.rearrange("(p j) c -> p j c", j=4))
 
         tab_rows = tab_scales.rearrange("a (q r) t -> r q a t", r=4)
         w2_rows = w2_scales.rearrange("a (q r) c -> r q a c", r=4)
         for r in range(4):
-            nc.scalar.dma_start(tab_sc[r:PARTS:16, :].bitcast(I32), tab_rows[r].bitcast(I32))
+            nc.sync.dma_start(tab_sc[r:PARTS:16, :].bitcast(I32), tab_rows[r].bitcast(I32))
+        load_w1(0, 0, AT_W1)
+        root_gain = held([PARTS, 2, 4], F32, "root_gain")
+        nc.scalar.activation(root_gain[:], gain_t[:, :, 0:4], ACT.Sqrt)
         load_tab(0)
+        w_sc = placed([PARTS, H], U8, "w_sc", AT_W_SC)
+        nc.vector.memset(w_sc[:].bitcast(I32), 0)
         for r in range(4):
-            nc.scalar.dma_start(w_sc[r:PARTS:16, :].bitcast(I32), w2_rows[r].bitcast(I32))
+            nc.sync.dma_start(w_sc[r:PARTS:16, :].bitcast(I32), w2_rows[r].bitcast(I32))
 
         for i in range(4):
             nc.vector.memset(pages[i][:], 0.0)
@@ -81,33 +86,21 @@ def tile_list_lens_fit_register_kernel(tc, tab_words, tab_scales, offs, w1, w2_w
 
         v_sc0 = held([PARTS, S], U8, "v_sc0")
         nc.vector.tensor_copy(v_sc0[:], tab_sc[:].indirect(scan_list[:]))
-        nc.scalar.dma_start(v_sc1[0:112, :].bitcast(I32), v_sc0[16:PARTS, :].bitcast(I32))
+        nc.sync.dma_start(v_sc1[0:112, :].bitcast(I32), v_sc0[16:PARTS, :].bitcast(I32))
         v_sc = [v_sc0, v_sc1]
 
         w2_dealt = held([PARTS, 4 * 4 * PARTS * 2], U8, "w2_dealt")
         nc.vector.tensor_copy(
             w2_dealt[:].bitcast(U16).rearrange("p (i g m) -> p g i m", i=4, m=8),
             w2_raw[:].rearrange("p a c -> p (a c)").bitcast(U16).rearrange("p (g m i) -> p g i m", i=4, m=8))
-        gain_t = early.tile([PARTS, 2, 4], F32, name="gain_t", offset=8192)
-        lift_t = early.tile([PARTS, 2, 4], F32, name="lift_t", offset=8224)
-        nc.sync.dma_start(gain_t[:], gain.rearrange("(b p i) -> p b i", b=2, i=4))
-        nc.sync.dma_start(lift_t[:], lift.rearrange("(b p i) -> p b i", b=2, i=4))
-        root_gain = held([PARTS, 8], F32, "root_gain")
-        nc.scalar.activation(root_gain[:], gain_t[:].rearrange("p b i -> p (b i)"), ACT.Sqrt)
-        load_w1(0, 0)
         load_tab(1)
-        load_w1(1, 0)
+        load_w1(1, 0, AT_SC + 4096)
         sc_dealt = held([PARTS, H], U8, "sc_dealt")
         nc.vector.tensor_copy(
             sc_dealt[:].rearrange("p (i g m) -> p g i m", i=4, m=16),
             w_sc[:].rearrange("p (g m i) -> p g i m", i=4, m=16))
-        nc.scalar.dma_start(w2_sc1[0:112, :].bitcast(I32), sc_dealt[16:PARTS, :].bitcast(I32))
+        nc.sync.dma_start(w2_sc1[0:112, :].bitcast(I32), sc_dealt[16:PARTS, :].bitcast(I32))
         w2_sc = [sc_dealt, w2_sc1]
-        w3_sc_raw = held([PARTS, N], U8, "w3_sc_raw", "w_sc")
-        nc.vector.memset(w3_sc_raw[:].bitcast(I32), 0)
-        for q in range(4):
-            nc.sync.dma_start(w3_sc_raw[32 * q:32 * q + 8, :].bitcast(I32),
-                              w3_scales[:, 4 * q:4 * q + 4, :].bitcast(I32))
 
         v = {}
 
@@ -121,7 +114,11 @@ def tile_list_lens_fit_register_kernel(tc, tab_words, tab_scales, offs, w1, w2_w
         w1_bf = {}
 
         def cast_w1(a, b, u, on_vector):
-            w1_bf[a, b, u] = ring.tile([PARTS, 2 * PARTS * 4], BF16, name="w1_bf", align_bytes=64)
+            if b == 0:
+                w1_bf[a, b, u] = held([PARTS, 2 * PARTS * 4], BF16, "w1_bf%d%d" % (a, u))
+            else:
+                w1_bf[a, b, u] = placed([PARTS, 2 * PARTS * 4], BF16, "w1_bf_late%d%d" % (a, u),
+                                        AT_H + 4096 * a + 2048 * u)
             dst = w1_bf[a, b, u][:].rearrange("p (i m j) -> p m i j", i=2, j=4)
             src = w1_raw[a, b][:].rearrange("p j (m i) -> p m i j", i=4)[:, :, 2 * u:2 * u + 2, :]
             if on_vector:
@@ -162,10 +159,10 @@ def tile_list_lens_fit_register_kernel(tc, tab_words, tab_scales, offs, w1, w2_w
         z_sc = {}
 
         def square(b, i):
-            h[b, i] = ring.tile([PARTS, S], F32, name="h", align_bytes=64)
+            h[b, i] = placed([PARTS, S], F32, "h%d%d" % (b, i), AT_H + 4096 * (4 * b + i))
             for s in range(2):
                 nc.scalar.activation(h[b, i][:, BANK * s:BANK * s + BANK], banks[b, i, s][:], ACT.Square,
-                                     scale=root_gain[:, 4 * b + i:4 * b + i + 1])
+                                     scale=root_gain[:, b, i:i + 1])
 
         def pick(b, i, halves):
             width = HALF * len(halves)
@@ -203,42 +200,51 @@ def tile_list_lens_fit_register_kernel(tc, tab_words, tab_scales, offs, w1, w2_w
                 pass_w1(1, b, i, stop=True)
             square(b, i)
 
-        gather_tab(0)
-        wgt_t = early.tile([PARTS, P], F32, name="wgt_t", offset=24640, align_bytes=64)
-        nc.sync.dma_start(wgt_t[:], wgt)
         for u in range(2):
             cast_w1(0, 0, u, False)
             quant_w1(0, 0, u)
-        load_w1(0, 1)
+        gather_tab(0)
+        wgt_t = placed([PARTS, P], F32, "wgt_t", AT_TAB0)
+        nc.sync.dma_start(wgt_t[:], wgt)
+        lift_t = placed([PARTS, 2, 8], F32, "lift_t", AT_TAB0 + 2048)
+        nc.sync.dma_start(lift_t[:, :, 0:4], lift.rearrange("(b p i) -> p b i", b=2, i=4))
+        load_w1(0, 1, AT_TAB0 + 4096)
+        load_w1(1, 1, AT_TAB0 + 12288)
         gather_tab(1)
+        w3_sc_raw = placed([PARTS, N], U8, "w3_sc_raw", AT_TAB1)
+        nc.vector.memset(w3_sc_raw[:].bitcast(I32), 0)
+        for q in range(4):
+            nc.sync.dma_start(w3_sc_raw[32 * q:32 * q + 8, :].bitcast(I32),
+                              w3_scales[:, 4 * q:4 * q + 4, :].bitcast(I32))
+        w3_raw = placed([PARTS, 2, N], U32, "w3_raw", AT_TAB1 + 1024)
+        nc.sync.dma_start(w3_raw[:].bitcast(I32), w3_words.rearrange("a p c i -> p a (c i)").bitcast(I32))
+        base_t = placed([PARTS, 4, P], F32, "base_t", AT_TAB1 + 6144)
+        nc.sync.dma_start(base_t[:], base.rearrange("(p i) m -> p i m", i=4))
+        wgo_t = placed([PARTS, P], F32, "wgo_t", AT_TAB1 + 14336)
+        nc.sync.dma_start(wgo_t[:], wgo)
         cast_w1(1, 0, 0, True)
         cast_w1(1, 0, 1, False)
-        load_w1(1, 1)
         for u in range(2):
             quant_w1(1, 0, u)
         for i in range(4):
             stage_one(0, i)
-        for a in range(2):
-            for u in range(2):
-                cast_w1(a, 1, u, u == 0)
-                quant_w1(a, 1, u)
-        w3_raw = staged([PARTS, 2, N], U32, "w3_raw", 0)
-        nc.sync.dma_start(w3_raw[:].bitcast(I32), w3_words.rearrange("a p c i -> p a (c i)").bitcast(I32))
-        base_t = staged([PARTS, 4, P], F32, "base_t", 1)
-        nc.sync.dma_start(base_t[:], base.rearrange("(p i) m -> p i m", i=4))
         for i in range(4):
             pick(0, i, (0, 1))
+            if i < 2:
+                for u in range(2):
+                    cast_w1(i, 1, u, u == 0)
+                for u in range(2):
+                    quant_w1(i, 1, u)
+        for i in range(4):
             root(0, i, 0)
         for i in range(4):
             stage_one(1, i)
 
-        wgo_t = held([PARTS, P], F32, "wgo_t", "w2_dealt")
-        nc.sync.dma_start(wgo_t[:], wgo)
-        w3_sc = held([PARTS, N], U8, "w3_sc")
+        w3_sc = placed([PARTS, N], U8, "w3_sc", AT_H + 4096 * 2)
         nc.vector.tensor_copy(
             w3_sc[:].rearrange("p (i g m) -> p g i m", i=4, m=16),
             w3_sc_raw[:].rearrange("p (g m i) -> p g i m", i=4, m=16))
-        w3_dealt = held([PARTS, 2 * N], U32, "w3_dealt")
+        w3_dealt = placed([PARTS, 2 * N], U32, "w3_dealt", AT_H + 4096 * 3)
         nc.vector.tensor_copy(
             w3_dealt[:].bitcast(I32).rearrange("p (i g m) -> p g i m", i=4, m=4),
             w3_raw[:].rearrange("p a c -> p (a c)").bitcast(I32).rearrange("p (g m i) -> p g i m", i=4, m=4))

from contextlib import ExitStack

import concourse.mybir as mybir

K, H, N, T, S, P, T2 = 1024, 1024, 512, 4096, 1024, 512, 1024
FLOPS = 2 * 2 * K * H * S + 2 * H * N * P

F32 = mybir.dt.float32
BF16 = mybir.dt.bfloat16
I32 = mybir.dt.int32
U32 = mybir.dt.uint32
U16 = mybir.dt.uint16
U8 = mybir.dt.uint8
E4M3 = mybir.dt.float8_e4m3fn_x4
E2M1 = mybir.dt.float4_e2m1fn_x4
ACT = mybir.ActivationFunctionType
ALU = mybir.AluOpType

PARTS = 128
BANK = 512
AT_W1, AT_TAB1, AT_W_SC, AT_TAB0, AT_SC, AT_H = 0, 8192, 24576, 25600, 41984, 54272
HALF = P // 2


def tile_list_lens_fit_register_kernel(tc, tab_words, tab_scales, offs, w1, w2_words, w2_scales, gain,
                                                 offs2, wgt, lift, w3_words, w3_scales, base, offs3, wgo, out):
    nc = tc.nc
    with ExitStack() as ctx:
        keep = ctx.enter_context(tc.tile_pool(name="keep", bufs=1))
        early = ctx.enter_context(tc.tile_pool(name="early", bufs=1))
        psum = ctx.enter_context(tc.psum_pool(name="psum", bufs=1))

        def held(shape, dtype, name, tag=None):
            return keep.tile(shape, dtype, name=name, tag=tag or name, align_bytes=64)

        def placed(shape, dtype, name, offset):
            return early.tile(shape, dtype, name=name, offset=offset, align_bytes=64)

        scan_list = held([PARTS, S // 16], U16, "scan_list")
        pick_lists = held([PARTS, P // 16], U16, "pick_lists")
        file_lists = held([PARTS, P // 16], U16, "file_lists")

        tab_sc = placed([PARTS, T], U8, "tab_sc", AT_SC + 4096)
        v_sc1 = held([PARTS, S], U8, "v_sc1")
        w2_sc1 = held([PARTS, H], U8, "w2_sc1")
        pages = [held([PARTS, T2], F32, "page%d" % i) for i in range(4)]
        nc.vector.memset(tab_sc[:].bitcast(I32), 0)
        nc.vector.memset(v_sc1[:].bitcast(I32), 0)
        nc.vector.memset(w2_sc1[:].bitcast(I32), 0)

        nc.sync.dma_start(scan_list[:], offs)
        gain_t = placed([PARTS, 2, 16], F32, "gain_t", AT_TAB0 - 64)
        nc.sync.dma_start(gain_t[:, :, 0:4], gain.rearrange("(b p i) -> p b i", b=2, i=4))
        nc.sync.dma_start(pick_lists[:], offs2)
        nc.sync.dma_start(file_lists[:], offs3)
        w2_raw = placed([PARTS, 2, 2 * H], U8, "w2_raw", AT_TAB1)
        nc.sync.dma_start(w2_raw[:].bitcast(I32), w2_words.rearrange("a p c -> p a c").bitcast(I32))
        tab = {}
        w1_raw = {}

        def load_tab(a):
            tab[a] = placed([PARTS, T], U32, "tab%d" % a, (AT_TAB0, AT_TAB1)[a])
            nc.sync.dma_start(tab[a][:].bitcast(I32), tab_words[a].rearrange("p t i -> p (t i)").bitcast(I32))

        def load_w1(a, b, offset):
            w1_raw[a, b] = placed([PARTS, 4, BANK], F32, "w1_raw%d%d" % (a, b), offset)
            rows = w1[512 * a:512 * a + 512, 512 * b:512 * b + 512]
            nc.sync.dma_start(w1_raw[a, b][:], rows.rearrange("(p j) c -> p j c", j=4))

        tab_rows = tab_scales.rearrange("a (q r) t -> r q a t", r=4)
        w2_rows = w2_scales.rearrange("a (q r) c -> r q a c", r=4)
        for r in range(4):
            nc.sync.dma_start(tab_sc[r:PARTS:16, :].bitcast(I32), tab_rows[r].bitcast(I32))
        load_w1(0, 0, AT_W1)
        root_gain = held([PARTS, 2, 4], F32, "root_gain")
        nc.scalar.activation(root_gain[:], gain_t[:, :, 0:4], ACT.Sqrt)
        load_tab(0)
        w_sc = placed([PARTS, H], U8, "w_sc", AT_W_SC)
        nc.vector.memset(w_sc[:].bitcast(I32), 0)
        for r in range(4):
            nc.sync.dma_start(w_sc[r:PARTS:16, :].bitcast(I32), w2_rows[r].bitcast(I32))

        for i in range(4):
            nc.vector.memset(pages[i][:], 0.0)


        v_sc0 = held([PARTS, S], U8, "v_sc0")
        nc.vector.tensor_copy(v_sc0[:], tab_sc[:].indirect(scan_list[:]))
        nc.sync.dma_start(v_sc1[0:112, :].bitcast(I32), v_sc0[16:PARTS, :].bitcast(I32))
        v_sc = [v_sc0, v_sc1]

        w2_dealt = held([PARTS, 4 * 4 * PARTS * 2], U8, "w2_dealt")
        nc.vector.tensor_copy(
            w2_dealt[:].bitcast(U16).rearrange("p (i g m) -> p g i m", i=4, m=8),
            w2_raw[:].rearrange("p a c -> p (a c)").bitcast(U16).rearrange("p (g m i) -> p g i m", i=4, m=8))
        load_tab(1)
        load_w1(1, 0, AT_SC + 4096)
        sc_dealt = held([PARTS, H], U8, "sc_dealt")
        nc.vector.tensor_copy(
            sc_dealt[:].rearrange("p (i g m) -> p g i m", i=4, m=16),
            w_sc[:].rearrange("p (g m i) -> p g i m", i=4, m=16))
        nc.sync.dma_start(w2_sc1[0:112, :].bitcast(I32), sc_dealt[16:PARTS, :].bitcast(I32))
        w2_sc = [sc_dealt, w2_sc1]

        v = {}

        def gather_tab(a):
            for s in range(2):
                v[a, s] = held([PARTS, BANK], U32, "v%d%d" % (a, s))
                nc.vector.tensor_copy(v[a, s][:], tab[a][:].indirect(scan_list[:, 32 * s:32 * s + 32]))

        w1_codes = {}
        w1_sc = {}
        w1_bf = {}

        def cast_w1(a, b, u, on_vector):
            if b == 0:
                w1_bf[a, b, u] = held([PARTS, 2 * PARTS * 4], BF16, "w1_bf%d%d" % (a, u))
            else:
                w1_bf[a, b, u] = placed([PARTS, 2 * PARTS * 4], BF16, "w1_bf_late%d%d" % (a, u),
                                        AT_H + 4096 * a + 2048 * u)
            dst = w1_bf[a, b, u][:].rearrange("p (i m j) -> p m i j", i=2, j=4)
            src = w1_raw[a, b][:].rearrange("p j (m i) -> p m i j", i=4)[:, :, 2 * u:2 * u + 2, :]
            if on_vector:
                nc.vector.tensor_scalar(dst, src, -1.0, None, ALU.mult)
            else:
                nc.scalar.activation(dst, src, ACT.Copy, scale=-1.0)

        def quant_w1(a, b, u):
            w1_codes[a, b, u] = held([PARTS, 2 * PARTS], U32, "w1_codes%d%d%d" % (a, b, u))
            w1_sc[a, b, u] = held([PARTS, 2 * PARTS], U8, "w1_sc%d%d%d" % (a, b, u))
            nc.vector.quantize_mx(w1_codes[a, b, u][:].bitcast(E4M3), w1_sc[a, b, u][:], w1_bf[a, b, u][:])

        banks = {}

        def pass_w2(a, b, i, stop=False):
            c = PARTS * (4 * i + 2 * a + b)
            cs = PARTS * (2 * i + b)
            for s in range(2):
                if a == 0:
                    banks[b, i, s] = psum.tile([PARTS, BANK], F32, name="bank%d" % (2 * i + s))
                cols = slice(BANK * s, BANK * s + BANK)
                nc.tensor.matmul_mx(banks[b, i, s][:], lhsT=w2_dealt[:, 2 * c:2 * c + 2 * PARTS].bitcast(E2M1),
                                    lhsT_scale=w2_sc[a][:, cs:cs + PARTS], rhs=v[a, s][:].bitcast(E4M3),
                                    rhs_scale=v_sc[a][:, cols], start=(a == 0), stop=stop)

        def pass_w1(a, b, i, stop=False):
            u, c = i // 2, PARTS * (i % 2)
            for s in range(2):
                cols = slice(BANK * s, BANK * s + BANK)
                nc.tensor.matmul_mx(banks[b, i, s][:], lhsT=w1_codes[a, b, u][:, c:c + PARTS].bitcast(E4M3),
                                    lhsT_scale=w1_sc[a, b, u][:, c:c + PARTS], rhs=v[a, s][:].bitcast(E4M3),
                                    rhs_scale=v_sc[a][:, cols], start=False, stop=stop)

        h = {}
        x = {}
        z_planes = {}
        z_codes = {}
        z_sc = {}

        def square(b, i):
            h[b, i] = placed([PARTS, S], F32, "h%d%d" % (b, i), AT_H + 4096 * (4 * b + i))
            for s in range(2):
                nc.scalar.activation(h[b, i][:, BANK * s:BANK * s + BANK], banks[b, i, s][:], ACT.Square,
                                     scale=root_gain[:, b, i:i + 1])

        def pick(b, i, halves):
            width = HALF * len(halves)
            picked = held([PARTS, width], F32, "x%d%d%d" % (b, i, halves[0]))
            m0 = HALF * halves[0]
            nc.vector.tensor_tensor(picked[:], h[b, i][:].indirect(pick_lists[:, m0 // 16:(m0 + width) // 16]),
                                    wgt_t[:, m0:m0 + width], ALU.mult)
            for n, c in enumerate(halves):
                x[b, i, c] = picked[:, HALF * n:HALF * n + HALF]

        def root(b, i, c):
            if i == 0:
                z_planes[b, c] = held([PARTS, 4, HALF], BF16, "z_planes%d%d" % (b, c))
            nc.scalar.activation(z_planes[b, c][:, i, :], x[b, i, c], ACT.Sqrt, bias=lift_t[:, b, i:i + 1])

        def quant_z(b, c):
            z_bf = held([PARTS, HALF, 4], BF16, "z_bf%d%d" % (b, c))
            if c == 0:
                nc.vector.tensor_copy(z_bf[:], z_planes[b, c][:].rearrange("p i m -> p m i"))
            else:
                nc.scalar.copy(z_bf[:], z_planes[b, c][:].rearrange("p i m -> p m i"))
            z_codes[b, c] = held([PARTS, HALF], U32, "z_codes%d%d" % (b, c))
            z_sc[b, c] = held([PARTS, HALF], U8, "z_sc%d%d" % (b, c))
            nc.vector.quantize_mx(z_codes[b, c][:].bitcast(E4M3), z_sc[b, c][:],
                                  z_bf[:].rearrange("p m i -> p (m i)"))

        def stage_one(b, i):
            pass_w2(0, b, i)
            pass_w1(0, b, i)
            if b == 0 and i >= 2:
                pass_w1(1, b, i)
                pass_w2(1, b, i, stop=True)
            else:
                pass_w2(1, b, i)
                pass_w1(1, b, i, stop=True)
            square(b, i)

        for u in range(2):
            cast_w1(0, 0, u, False)
            quant_w1(0, 0, u)
        gather_tab(0)
        wgt_t = placed([PARTS, P], F32, "wgt_t", AT_TAB0)
        nc.sync.dma_start(wgt_t[:], wgt)
        lift_t = placed([PARTS, 2, 8], F32, "lift_t", AT_TAB0 + 2048)
        nc.sync.dma_start(lift_t[:, :, 0:4], lift.rearrange("(b p i) -> p b i", b=2, i=4))
        load_w1(0, 1, AT_TAB0 + 4096)
        load_w1(1, 1, AT_TAB0 + 12288)
        gather_tab(1)
        w3_sc_raw = placed([PARTS, N], U8, "w3_sc_raw", AT_TAB1)
        nc.vector.memset(w3_sc_raw[:].bitcast(I32), 0)
        for q in range(4):
            nc.sync.dma_start(w3_sc_raw[32 * q:32 * q + 8, :].bitcast(I32),
                              w3_scales[:, 4 * q:4 * q + 4, :].bitcast(I32))
        w3_raw = placed([PARTS, 2, N], U32, "w3_raw", AT_TAB1 + 1024)
        nc.sync.dma_start(w3_raw[:].bitcast(I32), w3_words.rearrange("a p c i -> p a (c i)").bitcast(I32))
        base_t = placed([PARTS, 4, P], F32, "base_t", AT_TAB1 + 6144)
        nc.sync.dma_start(base_t[:], base.rearrange("(p i) m -> p i m", i=4))
        wgo_t = placed([PARTS, P], F32, "wgo_t", AT_TAB1 + 14336)
        nc.sync.dma_start(wgo_t[:], wgo)
        cast_w1(1, 0, 0, True)
        cast_w1(1, 0, 1, False)
        for u in range(2):
            quant_w1(1, 0, u)
        for i in range(4):
            stage_one(0, i)
        for i in range(4):
            pick(0, i, (0, 1))
            if i < 2:
                for u in range(2):
                    cast_w1(i, 1, u, u == 0)
                for u in range(2):
                    quant_w1(i, 1, u)
        for i in range(4):
            root(0, i, 0)
        for i in range(4):
            stage_one(1, i)

        w3_sc = placed([PARTS, N], U8, "w3_sc", AT_H + 4096 * 2)
        nc.vector.tensor_copy(
            w3_sc[:].rearrange("p (i g m) -> p g i m", i=4, m=16),
            w3_sc_raw[:].rearrange("p (g m i) -> p g i m", i=4, m=16))
        w3_dealt = placed([PARTS, 2 * N], U32, "w3_dealt", AT_H + 4096 * 3)
        nc.vector.tensor_copy(
            w3_dealt[:].bitcast(I32).rearrange("p (i g m) -> p g i m", i=4, m=4),
            w3_raw[:].rearrange("p a c -> p (a c)").bitcast(I32).rearrange("p (g m i) -> p g i m", i=4, m=4))
        quant_z(0, 0)
        for i in range(4):
            pick(1, i, (0,))
            root(1, i, 0)
        quant_z(1, 0)

        out_rows = out.rearrange("(p i) c -> p i c", i=4)
        y = {}

        def fit(c):
            acc = [psum.tile([PARTS, HALF], F32, name="bank%d" % (4 * c + i)) for i in range(4)]
            for b in range(2):
                for i in range(4):
                    w = PARTS * (2 * i + b)
                    nc.tensor.matmul_mx(acc[i][:], lhsT=w3_dealt[:, w:w + PARTS].bitcast(E4M3),
                                        lhsT_scale=w3_sc[4 * b:PARTS, PARTS * i:PARTS * i + PARTS],
                                        rhs=z_codes[b, c][:].bitcast(E4M3), rhs_scale=z_sc[b, c][:],
                                        start=(b == 0), stop=(b == 1))
            return acc

        def depart(acc, i, c):
            y[i, c] = held([PARTS, HALF], F32, "y%d%d" % (i, c), "z_bf11" if (i, c) == (3, 0) else None)
            nc.vector.tensor_tensor(y[i, c][:], acc[i][:], base_t[:, i, HALF * c:HALF * c + HALF], ALU.subtract)

        def file_away(i, c):
            m0 = HALF * c
            nc.vector.tensor_tensor(pages[i][:].indirect(file_lists[:, m0 // 16:(m0 + HALF) // 16]), y[i, c][:],
                                    wgo_t[:, m0:m0 + HALF], ALU.mult)

        acc0 = fit(0)
        for i in range(3):
            depart(acc0, i, 0)
        for i in range(4):
            pick(1, i, (1,))
        for b in range(2):
            for i in range(4):
                root(b, i, 1)
            quant_z(b, 1)
        acc1 = fit(1)
        depart(acc0, 3, 0)
        for i in range(4):
            file_away(i, 0)
        for i in range(4):
            depart(acc1, i, 1)
        for i in range(4):
            file_away(i, 1)
            nc.sync.dma_start(out_rows[:, i, :], pages[i][:])
